import numpy as np
import ml_dtypes


def mxq(x, axis, fmt="e4m3"):
    dtype, down = {"e4m3": (ml_dtypes.float8_e4m3fn, 7), "e5m2": (ml_dtypes.float8_e5m2, 14)}[fmt]
    v = np.moveaxis(np.asarray(x, np.float32).astype(ml_dtypes.bfloat16).astype(np.float64), axis, -1)
    blocks = v.reshape(v.shape[:-1] + (-1, 32))
    amax = np.abs(blocks).max(-1, keepdims=True)
    byte = np.maximum(np.where(amax > 0, np.frexp(amax)[1] - 1 + 127, 0) - down, 1)
    scale = np.exp2(byte - 127.0)
    codes = (blocks / scale).astype(np.float32).astype(dtype).astype(np.float64)
    return np.moveaxis((codes * scale).reshape(v.shape), -1, axis)


WIDE = False


def mx_kscale(k):
    if not WIDE:
        return np.ones(k)
    levels = np.array([10, -10, 5, -5, 0])
    if k % 512:
        return np.exp2(np.random.permutation(np.resize(levels, k // 32))).repeat(32)
    a = np.empty((k // 512, 16))
    for p in range(k // 512):
        a[p, :8] = np.random.permutation(np.resize(levels, 8))
        for g in range(8):
            far = levels[np.abs(levels - a[p, g]) >= 10]
            a[p, g + 8] = far[np.random.randint(len(far))]
    return np.exp2(a.ravel()).repeat(32)


def f64(x):
    return np.asarray(x).astype(np.float64)


def striped(idx):
    return np.tile(idx.reshape(-1, 16).T, (8, 1)).astype(np.uint16)


def unstriped(offs):
    return offs[:16].T.reshape(-1).astype(np.int64)


E2M1 = np.array([0.0, 0.5, 1.0, 1.5, 2.0, 3.0, 4.0, 6.0, -0.0, -0.5, -1.0, -1.5, -2.0, -3.0, -4.0, -6.0])


def pack_weight(w, fmt):
    k, n = w.shape
    w = f64(np.asarray(w, np.float32).astype(ml_dtypes.bfloat16)).reshape(k // 32, 32, n)
    amax = np.abs(w).max(1)
    if fmt == "e4m3":
        byte = np.frexp(amax)[1] - 1 + 127 - 7
    else:
        mant, ex = np.frexp(amax / 6.0)
        byte = np.where(mant > 0.5, ex, ex - 1) + 127
    byte = np.clip(np.where(amax > 0, byte, 1), 1, 254)
    scaled = (w * np.exp2(127.0 - byte)[:, None, :]).reshape(k, n).astype(np.float32)
    by_word = np.ascontiguousarray(scaled.reshape(k // 512, 128, 4, n).transpose(0, 1, 3, 2))
    if fmt == "e4m3":
        words = by_word.astype(ml_dtypes.float8_e4m3fn).view(np.uint8)
    else:
        c = by_word.astype(ml_dtypes.float4_e2m1fn).view(np.uint8) & 0xF
        words = (c[..., 0::2] | (c[..., 1::2] << 4)).reshape(k // 512, 128, 2 * n)
    return np.ascontiguousarray(words), np.ascontiguousarray(byte.astype(np.uint8).reshape(k // 512, 16, n))


def unpack_weight(words, scales, fmt):
    g, _, n = scales.shape
    words = np.ascontiguousarray(words).reshape(g, 128, n, -1)
    if fmt == "e4m3":
        vals = words.view(ml_dtypes.float8_e4m3fn).astype(np.float64)
    else:
        nib = np.empty((g, 128, n, 4), np.uint8)
        nib[..., 0::2] = words & 0xF
        nib[..., 1::2] = words >> 4
        vals = E2M1[nib]
    vals = vals * np.repeat(np.exp2(scales.astype(np.float64) - 127.0), 8, axis=1)[..., None]
    return vals.transpose(0, 1, 3, 2).reshape(g * 512, n)


def gelu(v):
    return 0.5 * v * (1.0 + np.tanh(np.sqrt(2.0 / np.pi) * (v + 0.044715 * v**3)))


K, T, S, H, T3, S2, P = 512, 4096, 1024, 1024, 2048, 512, 512


def setup_inputs():
    n = np.random.standard_normal
    s = mx_kscale(K)[:, None]
    u = mx_kscale(H)[:, None]
    d = {}
    d["tab_words"], d["tab_scales"] = pack_weight(n((K, T)) * s, "e4m3")
    d["offs"] = striped(np.random.permutation(T)[:S])
    d["w1"] = (n((K, H)) / s * u.T / K ** 0.5).astype(np.float32)
    d["w4_words"], d["w4_scales"] = pack_weight(n((K, H)) / s * u.T / K ** 0.5, "e2m1")
    d["w8_words"], d["w8_scales"] = pack_weight(n((K, H)) / s * u.T / K ** 0.5, "e4m3")
    d["least"] = (0.7 * n(H) * u[:, 0]).astype(np.float32)
    d["tab2_words"], d["tab2_scales"] = pack_weight(n((H, T3)) / u / H ** 0.5, "e4m3")
    d["offs2"] = striped(np.random.permutation(T3)[:S2])
    d["pos1"] = striped(np.random.permutation(S)[:P])
    d["pos2"] = striped(np.random.permutation(S)[:P])
    d["std"] = np.random.uniform(-1.0, 0.5, S2).astype(np.float32)
    return d


def reference(tab_words, tab_scales, offs, w1, w4_words, w4_scales, w8_words, w8_scales,
              least, tab2_words, tab2_scales, offs2, pos1, pos2, std):
    v = unpack_weight(tab_words, tab_scales, "e4m3")[:, unstriped(offs)]
    v2 = unpack_weight(tab2_words, tab2_scales, "e4m3")[:, unstriped(offs2)]
    low = f64(least)[:, None]
    a = mxq(f64(w1), 0, "e4m3").T @ v
    b = unpack_weight(w4_words, w4_scales, "e2m1").T @ v
    c = unpack_weight(w8_words, w8_scales, "e4m3").T @ v
    first = np.maximum(a, low)
    second = np.maximum(first + b, low)
    h = second + c
    e = v2.T @ mxq(h, 0, "e4m3")
    challenger = e[:, unstriped(pos1)]
    champion = e[:, unstriped(pos2)]
    return challenger - f64(std)[:, None] * np.maximum(challenger, champion)

@@ -1,0 +1,254 @@
+from contextlib import ExitStack
+
+import concourse.mybir as mybir
+
+K, T, S, H, T3, S2, NP = 512, 4096, 1024, 1024, 2048, 512, 512
+FLOPS = 2 * K * H * S * 3 + 2 * H * S2 * S
+
+F32 = mybir.dt.float32
+BF16 = mybir.dt.bfloat16
+I32 = mybir.dt.int32
+U32 = mybir.dt.uint32
+U16 = mybir.dt.uint16
+U8 = mybir.dt.uint8
+FP8X4 = mybir.dt.float8_e4m3fn_x4
+FP4X4 = mybir.dt.float4_e2m1fn_x4
+ALU = mybir.AluOpType
+ACT = mybir.ActivationFunctionType
+
+P = 128
+N = 512
+
+
+def tile_list_breed_ring_scores_kernel(
+    tc, tab_words, tab_scales, offs, w1, w4_words, w4_scales, w8_words, w8_scales,
+    least, tab2_words, tab2_scales, offs2, pos1, pos2, std, out,
+):
+    nc = tc.nc
+    with ExitStack() as ctx:
+        lists = ctx.enter_context(tc.tile_pool(name="lists", bufs=1))
+        keep = ctx.enter_context(tc.tile_pool(name="keep", bufs=1))
+        ring = ctx.enter_context(tc.tile_pool(name="ring", bufs=4))
+        pair = ctx.enter_context(tc.tile_pool(name="pair", bufs=2))
+        psum = ctx.enter_context(tc.psum_pool(name="psum", bufs=2))
+
+        offs_sb = lists.tile([P, S // 16], U16, name="offs_sb")
+        offs2_sb = lists.tile([P, S2 // 16], U16, name="offs2_sb")
+        pos1_sb = lists.tile([P, NP // 16], U16, name="pos1_sb")
+        pos2_sb = lists.tile([P, NP // 16], U16, name="pos2_sb")
+
+        def kept(shape, dtype, name):
+            return keep.tile(shape, dtype, name=name, align_bytes=64)
+
+        tab_w = kept([P, T], U32, "tab_w")
+        tab_s = kept([P, T], U8, "tab_s")
+        tab2_w = [kept([P, T3], U32, "tab2_w%d" % a) for a in range(2)]
+        tab2_s = kept([P, T3], U8, "tab2_s")
+        ws_raw = kept([P, H], U8, "ws_raw")
+        w8_raw = [kept([P, N], I32, "w8_raw%d" % b) for b in range(2)]
+        w4_raw = [kept([P, 2 * N], U8, "w4_raw%d" % b) for b in range(2)]
+        w1_raw = [kept([P, 4, N // 2], F32, "w1_raw%d" % i) for i in range(4)]
+        low = kept([P, 2, 4], F32, "low")
+        std_sb = kept([P, 4], F32, "std_sb")
+
+        w8_hbm = w8_words[0].rearrange("p n t -> p (n t)").bitcast(I32)
+        w4_hbm = w4_words[0].bitcast(I32)
+        w1_hbm = w1.rearrange("(p j) c -> p j c", j=4)
+
+        def load_weights(b):
+            nc.sync.dma_start(w8_raw[b][:], w8_hbm[:, b * N:(b + 1) * N])
+            nc.sync.dma_start(w4_raw[b][:].bitcast(I32), w4_hbm[:, b * N // 2:(b + 1) * N // 2])
+
+        def load_w1(i):
+            nc.sync.dma_start(w1_raw[i][:], w1_hbm[:, :, i * N // 2:(i + 1) * N // 2])
+
+        nc.gpsimd.memset(ws_raw[:].bitcast(I32), 0)
+        nc.sync.dma_start(offs_sb[:], offs)
+        tab_s_hbm = tab_scales[0].bitcast(I32)
+        for q in range(4):
+            nc.sync.dma_start(tab_s[32 * q:32 * q + 32, :].bitcast(I32),
+                              tab_s_hbm[4 * q:4 * q + 4, :].partition_broadcast(8))
+        nc.sync.dma_start(tab_w[:].bitcast(I32), tab_words[0].rearrange("p n t -> p (n t)").bitcast(I32))
+        load_w1(0)
+        load_w1(1)
+        w4s_hbm = w4_scales[0].bitcast(I32)
+        w8s_hbm = w8_scales[0].bitcast(I32)
+        for q in range(4):
+            nc.scalar.dma_start(ws_raw[32 * q:32 * q + 4, :].bitcast(I32), w4s_hbm[4 * q:4 * q + 4, :])
+            nc.gpsimd.dma_start(ws_raw[32 * q + 4:32 * q + 8, :].bitcast(I32), w8s_hbm[4 * q:4 * q + 4, :])
+        load_weights(0)
+        nc.sync.dma_start(low[:], least.rearrange("(b p t) -> p b t", b=2, t=4))
+        load_w1(2)
+        load_w1(3)
+        load_weights(1)
+        nc.sync.dma_start(offs2_sb[:], offs2)
+        nc.gpsimd.memset(tab2_s[:].bitcast(I32), 0)
+        tab2_s_hbm = tab2_scales.bitcast(I32)
+        for q in range(4):
+            nc.gpsimd.dma_start(tab2_s[32 * q:32 * q + 8, :].bitcast(I32), tab2_s_hbm[:, 4 * q:4 * q + 4, :])
+        for a in range(2):
+            nc.sync.dma_start(tab2_w[a][:].bitcast(I32), tab2_words[a].rearrange("p n t -> p (n t)").bitcast(I32))
+        nc.sync.dma_start(pos1_sb[:], pos1)
+        nc.sync.dma_start(pos2_sb[:], pos2)
+        with nc.allow_non_contiguous_dma(reason="one value of std for each partition"):
+            nc.sync.dma_start(std_sb[:], std.rearrange("(u p) -> p u", p=P))
+
+        v_s = kept([P, S], U8, "v_s")
+        nc.vector.tensor_copy(v_s[:], tab_s[:].indirect(offs_sb[:]))
+        v_w = [kept([P, N], U32, "v_w%d" % jc) for jc in range(2)]
+
+        def gather_v(jc):
+            nc.vector.tensor_copy(v_w[jc][:], tab_w[:].indirect(offs_sb[:, 32 * jc:32 * jc + 32]))
+
+        w1_bf = [kept([P, 4, P, 4], BF16, "w1_bf%d" % b) for b in range(2)]
+        w1_c = [kept([P, N], U32, "w1_c%d" % b) for b in range(2)]
+        w1_s = [kept([P, N], U8, "w1_s%d" % b) for b in range(2)]
+        w8_p = [kept([P, 4, P], I32, "w8_p%d" % b) for b in range(2)]
+        w4_p = [kept([P, 4, P], U16, "w4_p%d" % b) for b in range(2)]
+        ws_p = [kept([P, 4, P], U8, "ws_p%d" % b) for b in range(2)]
+
+        def prepare_weights(b):
+            for hf in range(2):
+                nc.scalar.copy(
+                    w1_bf[b][:, :, 64 * hf:64 * hf + 64, :].rearrange("p t m j -> p m j t"),
+                    w1_raw[2 * b + hf][:].rearrange("p j (m t) -> p m j t", t=4))
+            nc.vector.tensor_copy(ws_p[b][:].rearrange("p t q -> p q t"),
+                                  ws_raw[:, b * N:(b + 1) * N].rearrange("p (q t) -> p q t", t=4))
+            nc.vector.tensor_copy(w4_p[b][:].rearrange("p t q -> p q t"),
+                                  w4_raw[b][:].bitcast(U16).rearrange("p (q t) -> p q t", t=4))
+            nc.vector.tensor_copy(w8_p[b][:].rearrange("p t q -> p q t"),
+                                  w8_raw[b][:].rearrange("p (q t) -> p q t", t=4))
+            nc.vector.quantize_mx(out=w1_c[b][:].bitcast(FP8X4), scales=w1_s[b][:],
+                                  in_=w1_bf[b][:].rearrange("p t m j -> p (t m j)"))
+
+        v2_w = [kept([P, S2], U32, "v2_w%d" % a) for a in range(2)]
+        v2_s = kept([P, S2], U8, "v2_s")
+
+        def gather_v2():
+            nc.vector.tensor_copy(v2_s[:], tab2_s[:].indirect(offs2_sb[:]))
+            for a in range(2):
+                nc.vector.tensor_copy(v2_w[a][:], tab2_w[a][:].indirect(offs2_sb[:]))
+
+        h_c = [kept([P, N], U32, "h_c%d" % g) for g in range(4)]
+        h_s = [kept([P, N], U8, "h_s%d" % g) for g in range(4)]
+        e_sb = [kept([P, S], F32, "e_sb%d" % u) for u in range(4)]
+
+        state = {}
+
+        def product_b(i):
+            jc, b, t = i // 8, (i // 4) % 2, i % 4
+            bank_b = psum.tile([P, N], F32, name="bank_b")
+            nc.tensor.matmul_mx(out=bank_b[:], lhsT=w4_p[b][:, t, :].bitcast(FP4X4), lhsT_scale=ws_p[b][:, t, :],
+                                rhs=v_w[jc][:].bitcast(FP8X4), rhs_scale=v_s[:, jc * N:(jc + 1) * N],
+                                start=True, stop=True)
+            b_sb = ring.tile([P, N], F32, name="b_sb")
+            nc.scalar.copy(b_sb[:], bank_b[:])
+            state["b", i] = b_sb
+
+        def products(i):
+            jc, b, t = i // 8, (i // 4) % 2, i % 4
+            cols = slice(P * t, P * t + P)
+            rhs = v_w[jc][:].bitcast(FP8X4)
+            rhs_s = v_s[:, jc * N:(jc + 1) * N]
+            bank_a = psum.tile([P, N], F32, name="bank_a")
+            bank_c = psum.tile([P, N], F32, name="bank_c")
+            nc.tensor.matmul_mx(out=bank_a[:], lhsT=w1_c[b][:, cols].bitcast(FP8X4), lhsT_scale=w1_s[b][:, cols],
+                                rhs=rhs, rhs_scale=rhs_s, start=True, stop=True)
+            nc.tensor.matmul_mx(out=bank_c[:], lhsT=w8_p[b][:, t, :].bitcast(FP8X4), lhsT_scale=ws_p[b][4:P, t, :],
+                                rhs=rhs, rhs_scale=rhs_s, start=True, stop=True)
+            state["abc", i] = (bank_a, state["b", i], bank_c)
+
+        def first_sum(i):
+            b, t = (i // 4) % 2, i % 4
+            bank_a, b_sb, bank_c = state["abc", i]
+            run = ring.tile([P, N], F32, name="run")
+            nc.vector.scalar_tensor_tensor(run[:], bank_a[:], low[:, b, t:t + 1], b_sb[:], ALU.max, ALU.add)
+            state["run", i] = run
+
+        def second_sum(i):
+            g, b, t = i // 4, (i // 4) % 2, i % 4
+            if t == 0:
+                state["h_bf", g] = pair.tile([P, 4, N], BF16, name="h_bf")
+            nc.vector.scalar_tensor_tensor(state["h_bf", g][:, t, :], state["run", i][:], low[:, b, t:t + 1],
+                                           state["abc", i][2][:], ALU.max, ALU.add)
+
+        def weave(g, part):
+            if part == 0:
+                state["h_wv", g] = pair.tile([P, N, 4], BF16, name="h_wv", align_bytes=64)
+            cols = slice(P * part, P * part + P)
+            nc.scalar.copy(state["h_wv", g][:, cols, :].rearrange("p (c i) t -> p c t i", i=4),
+                           state["h_bf", g][:, :, cols].rearrange("p t (c i) -> p c t i", i=4))
+
+        def quantize_h(g):
+            nc.vector.quantize_mx(out=h_c[g][:].bitcast(FP8X4), scales=h_s[g][:],
+                                  in_=state["h_wv", g][:].rearrange("p n t -> p (n t)"))
+
+        def score_pass(jc, u, a):
+            if a == 0:
+                state["e", jc, u] = psum.tile([P, N], F32, name="bank_e")
+            cols = slice(P * u, P * u + P)
+            nc.tensor.matmul_mx(out=state["e", jc, u][:], lhsT=v2_w[a][:, cols].bitcast(FP8X4),
+                                lhsT_scale=v2_s[4 * a:P, cols], rhs=h_c[2 * jc + a][:].bitcast(FP8X4),
+                                rhs_scale=h_s[2 * jc + a][:], start=(a == 0), stop=(a == 1))
+            if a == 1:
+                nc.scalar.copy(e_sb[u][:, jc * N:(jc + 1) * N], state["e", jc, u][:])
+
+        gather_v(0)
+        gather_v(1)
+        prepare_weights(0)
+        product_b(0)
+        product_b(1)
+        products(0)
+        first_sum(0)
+        for i in range(16):
+            g, t = i // 4, i % 4
+            if i + 2 == 4:
+                prepare_weights(1)
+            if i + 2 < 16:
+                product_b(i + 2)
+            if i + 1 < 16:
+                products(i + 1)
+                first_sum(i + 1)
+            second_sum(i)
+            if g > 0:
+                weave(g - 1, t)
+                if t == 3:
+                    quantize_h(g - 1)
+            if i == 6:
+                gather_v2()
+            if g == 3:
+                score_pass(0, t, 0)
+                score_pass(0, t, 1)
+        for part in range(4):
+            weave(3, part)
+        quantize_h(3)
+
+        neg_std = kept([P, 4], F32, "neg_std")
+        rest = kept([P, 4], F32, "rest")
+        nc.gpsimd.tensor_scalar(neg_std[:], std_sb[:], -1.0, 0.0, ALU.mult, ALU.add)
+        nc.gpsimd.tensor_scalar(rest[:], std_sb[:], -1.0, 1.0, ALU.mult, ALU.add)
+
+        def pick(u):
+            score_pass(1, u, 0)
+            score_pass(1, u, 1)
+            chal = ring.tile([P, NP], F32, name="chal")
+            nc.vector.tensor_copy(chal[:], e_sb[u][:].indirect(pos1_sb[:]))
+            lead = ring.tile([P, NP], F32, name="lead")
+            nc.vector.tensor_tensor(lead[:], e_sb[u][:].indirect(pos2_sb[:]), chal[:], ALU.subtract)
+            own = ring.tile([P, NP], F32, name="own")
+            nc.scalar.activation(own[:], chal[:], ACT.Copy, scale=rest[:, u:u + 1])
+            over = ring.tile([P, NP], F32, name="over")
+            nc.scalar.activation(over[:], lead[:], ACT.Relu)
+            state["pick", u] = (own, over)
+
+        def finish(u):
+            own, over = state["pick", u]
+            res = ring.tile([P, NP], F32, name="res")
+            nc.vector.scalar_tensor_tensor(res[:], over[:], neg_std[:, u:u + 1], own[:], ALU.mult, ALU.add)
+            nc.sync.dma_start(out[P * u:P * u + P, :], res[:])
+
+        for u in range(4):
+            pick(u)
+            if u > 0:
+                finish(u - 1)
+        finish(3)

@@ -18,6 +18,8 @@ ACT = mybir.ActivationFunctionType
 
 P = 128
 N = 512
+RELIEF = ()
+GWEAVE = ()
 
 
 def tile_list_breed_ring_scores_kernel(
@@ -49,43 +51,48 @@ def tile_list_breed_ring_scores_kernel(
         w4_raw = [kept([P, 2 * N], U8, "w4_raw%d" % b) for b in range(2)]
         w1_raw = [kept([P, 4, N // 2], F32, "w1_raw%d" % i) for i in range(4)]
         low = kept([P, 2, 4], F32, "low")
+        neg_low = kept([P, 2, 4], F32, "neg_low")
         std_sb = kept([P, 4], F32, "std_sb")
 
         w8_hbm = w8_words[0].rearrange("p n t -> p (n t)").bitcast(I32)
         w4_hbm = w4_words[0].bitcast(I32)
         w1_hbm = w1.rearrange("(p j) c -> p j c", j=4)
+        tab_s_hbm = tab_scales[0].bitcast(I32)
+        tab2_s_hbm = tab2_scales.bitcast(I32)
+        w4s_hbm = w4_scales[0].bitcast(I32)
+        w8s_hbm = w8_scales[0].bitcast(I32)
 
         def load_weights(b):
-            nc.sync.dma_start(w8_raw[b][:], w8_hbm[:, b * N:(b + 1) * N])
             nc.sync.dma_start(w4_raw[b][:].bitcast(I32), w4_hbm[:, b * N // 2:(b + 1) * N // 2])
+            nc.sync.dma_start(w8_raw[b][:], w8_hbm[:, b * N:(b + 1) * N])
 
         def load_w1(i):
             nc.sync.dma_start(w1_raw[i][:], w1_hbm[:, :, i * N // 2:(i + 1) * N // 2])
 
-        nc.gpsimd.memset(ws_raw[:].bitcast(I32), 0)
+        def load_scale_rows(hbm, first, quads):
+            for q in quads:
+                nc.sync.dma_start(ws_raw[32 * q + first:32 * q + first + 4, :].bitcast(I32), hbm[4 * q:4 * q + 4, :])
+
+        nc.vector.memset(ws_raw[:].bitcast(I32), 0)
+        nc.gpsimd.memset(tab2_s[:].bitcast(I32), 0)
         nc.sync.dma_start(offs_sb[:], offs)
-        tab_s_hbm = tab_scales[0].bitcast(I32)
         for q in range(4):
             nc.sync.dma_start(tab_s[32 * q:32 * q + 32, :].bitcast(I32),
                               tab_s_hbm[4 * q:4 * q + 4, :].partition_broadcast(8))
+        load_scale_rows(w4s_hbm, 0, (0, 1))
         nc.sync.dma_start(tab_w[:].bitcast(I32), tab_words[0].rearrange("p n t -> p (n t)").bitcast(I32))
+        load_scale_rows(w4s_hbm, 0, (2, 3))
+        load_scale_rows(w8s_hbm, 4, (0, 1, 2, 3))
         load_w1(0)
         load_w1(1)
-        w4s_hbm = w4_scales[0].bitcast(I32)
-        w8s_hbm = w8_scales[0].bitcast(I32)
-        for q in range(4):
-            nc.scalar.dma_start(ws_raw[32 * q:32 * q + 4, :].bitcast(I32), w4s_hbm[4 * q:4 * q + 4, :])
-            nc.gpsimd.dma_start(ws_raw[32 * q + 4:32 * q + 8, :].bitcast(I32), w8s_hbm[4 * q:4 * q + 4, :])
         load_weights(0)
         nc.sync.dma_start(low[:], least.rearrange("(b p t) -> p b t", b=2, t=4))
         load_w1(2)
         load_w1(3)
         load_weights(1)
         nc.sync.dma_start(offs2_sb[:], offs2)
-        nc.gpsimd.memset(tab2_s[:].bitcast(I32), 0)
-        tab2_s_hbm = tab2_scales.bitcast(I32)
         for q in range(4):
-            nc.gpsimd.dma_start(tab2_s[32 * q:32 * q + 8, :].bitcast(I32), tab2_s_hbm[:, 4 * q:4 * q + 4, :])
+            nc.sync.dma_start(tab2_s[32 * q:32 * q + 8, :].bitcast(I32), tab2_s_hbm[:, 4 * q:4 * q + 4, :])
         for a in range(2):
             nc.sync.dma_start(tab2_w[a][:].bitcast(I32), tab2_words[a].rearrange("p n t -> p (n t)").bitcast(I32))
         nc.sync.dma_start(pos1_sb[:], pos1)
@@ -108,147 +115,221 @@ def tile_list_breed_ring_scores_kernel(
         ws_p = [kept([P, 4, P], U8, "ws_p%d" % b) for b in range(2)]
 
         def prepare_weights(b):
-            for hf in range(2):
-                nc.scalar.copy(
-                    w1_bf[b][:, :, 64 * hf:64 * hf + 64, :].rearrange("p t m j -> p m j t"),
-                    w1_raw[2 * b + hf][:].rearrange("p j (m t) -> p m j t", t=4))
+            for part in range(4):
+                dst = w1_bf[b][:, :, 32 * part:32 * part + 32, :].rearrange("p t m j -> p m j t")
+                src = w1_raw[2 * b + part // 2][:, :, 128 * (part % 2):128 * (part % 2) + 128]
+                src = src.rearrange("p j (m t) -> p m j t", t=4)
+                if b == 0 and part == 3:
+                    nc.vector.tensor_copy(dst, src)
+                elif b == 1 and False:
+                    nc.gpsimd.tensor_scalar(dst, src, 1.0, 0.0, ALU.mult, ALU.add)
+                else:
+                    nc.scalar.copy(dst, src)
             nc.vector.tensor_copy(ws_p[b][:].rearrange("p t q -> p q t"),
                                   ws_raw[:, b * N:(b + 1) * N].rearrange("p (q t) -> p q t", t=4))
             nc.vector.tensor_copy(w4_p[b][:].rearrange("p t q -> p q t"),
                                   w4_raw[b][:].bitcast(U16).rearrange("p (q t) -> p q t", t=4))
-            nc.vector.tensor_copy(w8_p[b][:].rearrange("p t q -> p q t"),
-                                  w8_raw[b][:].rearrange("p (q t) -> p q t", t=4))
-            nc.vector.quantize_mx(out=w1_c[b][:].bitcast(FP8X4), scales=w1_s[b][:],
-                                  in_=w1_bf[b][:].rearrange("p t m j -> p (t m j)"))
+            calls = 2 - b
+            wide = N // calls
+            for k in range(calls):
+                nc.vector.quantize_mx(out=w1_c[b][:, k * wide:(k + 1) * wide].bitcast(FP8X4),
+                                      scales=w1_s[b][:, k * wide:(k + 1) * wide],
+                                      in_=w1_bf[b][:].rearrange("p t m j -> p (t m j)")[:, 4 * k * wide:4 * (k + 1) * wide])
+                if k == 0:
+                    nc.vector.tensor_copy(w8_p[b][:].rearrange("p t q -> p q t"),
+                                          w8_raw[b][:].rearrange("p (q t) -> p q t", t=4))
 
-        v2_w = [kept([P, S2], U32, "v2_w%d" % a) for a in range(2)]
+        v2_w = {(a, 0): kept([P, S2 // 2], U32, "v2_w%d" % a) for a in range(2)}
         v2_s = kept([P, S2], U8, "v2_s")
 
         def gather_v2():
             nc.vector.tensor_copy(v2_s[:], tab2_s[:].indirect(offs2_sb[:]))
             for a in range(2):
-                nc.vector.tensor_copy(v2_w[a][:], tab2_w[a][:].indirect(offs2_sb[:]))
+                nc.vector.tensor_copy(v2_w[a, 0][:], tab2_w[a][:].indirect(offs2_sb[:, 0:16]))
+
+        def gather_v2_late():
+            late = keep.tile([P, 2, S2 // 2], U32, name="v2_late", tag="last_woven", align_bytes=64)
+            for a in range(2):
+                v2_w[a, 1] = late[:, a, :]
+                nc.vector.tensor_copy(late[:, a, :], tab2_w[a][:].indirect(offs2_sb[:, 16:32]))
 
         h_c = [kept([P, N], U32, "h_c%d" % g) for g in range(4)]
         h_s = [kept([P, N], U8, "h_s%d" % g) for g in range(4)]
         e_sb = [kept([P, S], F32, "e_sb%d" % u) for u in range(4)]
 
+        steps = [(g, t, 0, N) for g in range(3) for t in range(4)]
+        steps = steps + [(3, t, c0, N // 2) for c0 in (0, N // 2) for t in range(4)]
         state = {}
 
+        def moving(i):
+            g, t, c0, n = steps[i]
+            jc = g % 2
+            return v_w[jc][:, c0:c0 + n].bitcast(FP8X4), v_s[:, jc * N + c0:jc * N + c0 + n]
+
         def product_b(i):
-            jc, b, t = i // 8, (i // 4) % 2, i % 4
-            bank_b = psum.tile([P, N], F32, name="bank_b")
+            g, t, c0, n = steps[i]
+            b = g // 2
+            rhs, rhs_s = moving(i)
+            bank_b = psum.tile([P, n], F32, name="bank_b")
             nc.tensor.matmul_mx(out=bank_b[:], lhsT=w4_p[b][:, t, :].bitcast(FP4X4), lhsT_scale=ws_p[b][:, t, :],
-                                rhs=v_w[jc][:].bitcast(FP8X4), rhs_scale=v_s[:, jc * N:(jc + 1) * N],
-                                start=True, stop=True)
-            b_sb = ring.tile([P, N], F32, name="b_sb")
-            nc.scalar.copy(b_sb[:], bank_b[:])
+                                rhs=rhs, rhs_scale=rhs_s, start=True, stop=True)
+            b_sb = ring.tile([P, n], F32, name="b_sb")
+            if i in RELIEF:
+                nc.scalar.activation(b_sb[:], bank_b[:], ACT.Identity, bias=low[:, b, t:t + 1])
+            else:
+                nc.scalar.copy(b_sb[:], bank_b[:])
             state["b", i] = b_sb
 
-        def products(i):
-            jc, b, t = i // 8, (i // 4) % 2, i % 4
+        def product_a(i):
+            g, t, c0, n = steps[i]
+            b = g // 2
             cols = slice(P * t, P * t + P)
-            rhs = v_w[jc][:].bitcast(FP8X4)
-            rhs_s = v_s[:, jc * N:(jc + 1) * N]
-            bank_a = psum.tile([P, N], F32, name="bank_a")
-            bank_c = psum.tile([P, N], F32, name="bank_c")
+            rhs, rhs_s = moving(i)
+            bank_a = psum.tile([P, n], F32, name="bank_a")
             nc.tensor.matmul_mx(out=bank_a[:], lhsT=w1_c[b][:, cols].bitcast(FP8X4), lhsT_scale=w1_s[b][:, cols],
                                 rhs=rhs, rhs_scale=rhs_s, start=True, stop=True)
+            state["a", i] = bank_a
+
+        def product_c(i):
+            g, t, c0, n = steps[i]
+            b = g // 2
+            rhs, rhs_s = moving(i)
+            bank_c = psum.tile([P, n], F32, name="bank_c")
             nc.tensor.matmul_mx(out=bank_c[:], lhsT=w8_p[b][:, t, :].bitcast(FP8X4), lhsT_scale=ws_p[b][4:P, t, :],
                                 rhs=rhs, rhs_scale=rhs_s, start=True, stop=True)
-            state["abc", i] = (bank_a, state["b", i], bank_c)
+            state["c", i] = bank_c
 
         def first_sum(i):
-            b, t = (i // 4) % 2, i % 4
-            bank_a, b_sb, bank_c = state["abc", i]
-            run = ring.tile([P, N], F32, name="run")
-            nc.vector.scalar_tensor_tensor(run[:], bank_a[:], low[:, b, t:t + 1], b_sb[:], ALU.max, ALU.add)
+            g, t, c0, n = steps[i]
+            b = g // 2
+            run = ring.tile([P, n], F32, name="run")
+            if i in RELIEF:
+                above = ring.tile([P, n], F32, name="above")
+                nc.scalar.activation(above[:], state["a", i][:], ACT.Relu, bias=neg_low[:, b, t:t + 1])
+                nc.gpsimd.tensor_tensor(run[:], above[:], state["b", i][:], ALU.add)
+            else:
+                nc.vector.scalar_tensor_tensor(run[:], state["a", i][:], low[:, b, t:t + 1], state["b", i][:],
+                                               ALU.max, ALU.add)
             state["run", i] = run
 
         def second_sum(i):
-            g, b, t = i // 4, (i // 4) % 2, i % 4
-            if t == 0:
+            g, t, c0, n = steps[i]
+            b = g // 2
+            if t == 0 and c0 == 0:
                 state["h_bf", g] = pair.tile([P, 4, N], BF16, name="h_bf")
-            nc.vector.scalar_tensor_tensor(state["h_bf", g][:, t, :], state["run", i][:], low[:, b, t:t + 1],
-                                           state["abc", i][2][:], ALU.max, ALU.add)
+            nc.vector.scalar_tensor_tensor(state["h_bf", g][:, t, c0:c0 + n], state["run", i][:], low[:, b, t:t + 1],
+                                           state["c", i][:], ALU.max, ALU.add)
 
-        def weave(g, part):
-            if part == 0:
+        def weave(g, part, on_vector):
+            if part == 0 and g == 3:
+                state["h_wv", g] = keep.tile([P, N, 4], BF16, name="h_wv_last", tag="last_woven", align_bytes=64)
+            elif part == 0:
                 state["h_wv", g] = pair.tile([P, N, 4], BF16, name="h_wv", align_bytes=64)
             cols = slice(P * part, P * part + P)
-            nc.scalar.copy(state["h_wv", g][:, cols, :].rearrange("p (c i) t -> p c t i", i=4),
-                           state["h_bf", g][:, :, cols].rearrange("p t (c i) -> p c t i", i=4))
+            dst = state["h_wv", g][:, cols, :].rearrange("p (c i) t -> p c t i", i=4)
+            src = state["h_bf", g][:, :, cols].rearrange("p t (c i) -> p c t i", i=4)
+            if on_vector:
+                nc.vector.tensor_copy(dst, src)
+            elif 4 * g + part in GWEAVE:
+                nc.gpsimd.tensor_scalar(dst, src, 1.0, 0.0, ALU.mult, ALU.add)
+            else:
+                nc.scalar.copy(dst, src)
 
-        def quantize_h(g):
-            nc.vector.quantize_mx(out=h_c[g][:].bitcast(FP8X4), scales=h_s[g][:],
-                                  in_=state["h_wv", g][:].rearrange("p n t -> p (n t)"))
+        def quantize_h(g, c0, n):
+            nc.vector.quantize_mx(out=h_c[g][:, c0:c0 + n].bitcast(FP8X4), scales=h_s[g][:, c0:c0 + n],
+                                  in_=state["h_wv", g][:, c0:c0 + n, :].rearrange("p n t -> p (n t)"))
 
-        def score_pass(jc, u, a):
-            if a == 0:
-                state["e", jc, u] = psum.tile([P, N], F32, name="bank_e")
+        def score_pass(bank, u, jc, c0, n, a):
             cols = slice(P * u, P * u + P)
-            nc.tensor.matmul_mx(out=state["e", jc, u][:], lhsT=v2_w[a][:, cols].bitcast(FP8X4),
-                                lhsT_scale=v2_s[4 * a:P, cols], rhs=h_c[2 * jc + a][:].bitcast(FP8X4),
-                                rhs_scale=h_s[2 * jc + a][:], start=(a == 0), stop=(a == 1))
-            if a == 1:
-                nc.scalar.copy(e_sb[u][:, jc * N:(jc + 1) * N], state["e", jc, u][:])
+            g = 2 * a + jc
+            nc.tensor.matmul_mx(out=bank[:], lhsT=v2_w[a, u // 2][:, P * (u % 2):P * (u % 2) + P].bitcast(FP8X4),
+                                lhsT_scale=v2_s[4 * a:P, cols], rhs=h_c[g][:, c0:c0 + n].bitcast(FP8X4),
+                                rhs_scale=h_s[g][:, c0:c0 + n], start=(a == 0), stop=(a == 1))
 
+        def scores(u, jc, c0, n):
+            bank_e = psum.tile([P, n], F32, name="bank_e")
+            score_pass(bank_e, u, jc, c0, n, 0)
+            score_pass(bank_e, u, jc, c0, n, 1)
+            nc.scalar.copy(e_sb[u][:, jc * N + c0:jc * N + c0 + n], bank_e[:])
+
+        nc.gpsimd.tensor_scalar(neg_low[:], low[:], -1.0, 0.0, ALU.mult, ALU.add)
         gather_v(0)
         gather_v(1)
         prepare_weights(0)
-        product_b(0)
-        product_b(1)
-        products(0)
-        first_sum(0)
-        for i in range(16):
-            g, t = i // 4, i % 4
-            if i + 2 == 4:
+        LEAD = 1
+        for i in range(LEAD + 1):
+            product_b(i)
+        for i in range(LEAD):
+            product_a(i)
+            first_sum(i)
+        product_c(0)
+        last = len(steps) - 1
+        for i in range(len(steps)):
+            g, t, c0, n = steps[i]
+            if i == 4:
                 prepare_weights(1)
-            if i + 2 < 16:
-                product_b(i + 2)
-            if i + 1 < 16:
-                products(i + 1)
-                first_sum(i + 1)
+            if i + LEAD + 1 <= last:
+                product_b(i + LEAD + 1)
+            if i + LEAD <= last:
+                product_a(i + LEAD)
+                first_sum(i + LEAD)
+            if i + 1 <= last:
+                product_c(i + 1)
             second_sum(i)
-            if g > 0:
-                weave(g - 1, t)
+            if g > 0 and c0 == 0:
+                weave(g - 1, t, False)
                 if t == 3:
-                    quantize_h(g - 1)
-            if i == 6:
+                    quantize_h(g - 1, 0, N)
+            if c0 > 0 and t < 2:
+                weave(3, t, False)
+            if c0 > 0 and t == 2:
+                quantize_h(3, 0, N // 2)
+                scores(0, 0, 0, N)
+                scores(0, 1, 0, N // 2)
+            if i == 9:
                 gather_v2()
-            if g == 3:
-                score_pass(0, t, 0)
-                score_pass(0, t, 1)
-        for part in range(4):
-            weave(3, part)
-        quantize_h(3)
+        weave(3, 2, True)
+        weave(3, 3, False)
+        quantize_h(3, N // 2, N // 2)
+        gather_v2_late()
 
         neg_std = kept([P, 4], F32, "neg_std")
         rest = kept([P, 4], F32, "rest")
         nc.gpsimd.tensor_scalar(neg_std[:], std_sb[:], -1.0, 0.0, ALU.mult, ALU.add)
         nc.gpsimd.tensor_scalar(rest[:], std_sb[:], -1.0, 1.0, ALU.mult, ALU.add)
 
-        def pick(u):
-            score_pass(1, u, 0)
-            score_pass(1, u, 1)
+        def pick(u, pieces):
             chal = ring.tile([P, NP], F32, name="chal")
             nc.vector.tensor_copy(chal[:], e_sb[u][:].indirect(pos1_sb[:]))
-            lead = ring.tile([P, NP], F32, name="lead")
-            nc.vector.tensor_tensor(lead[:], e_sb[u][:].indirect(pos2_sb[:]), chal[:], ALU.subtract)
             own = ring.tile([P, NP], F32, name="own")
             nc.scalar.activation(own[:], chal[:], ACT.Copy, scale=rest[:, u:u + 1])
-            over = ring.tile([P, NP], F32, name="over")
-            nc.scalar.activation(over[:], lead[:], ACT.Relu)
-            state["pick", u] = (own, over)
+            n = NP // pieces
+            for k in range(pieces):
+                lead = ring.tile([P, n], F32, name="lead")
+                if pieces == 1:
+                    places = pos2_sb[:]
+                else:
+                    places = pos2_sb[:, k * n // 16:(k + 1) * n // 16]
+                nc.vector.tensor_tensor(lead[:], e_sb[u][:].indirect(places), chal[:, k * n:(k + 1) * n], ALU.subtract)
+                over = ring.tile([P, n], F32, name="over")
+                nc.scalar.activation(over[:], lead[:], ACT.Relu)
+                state["pick", u, k] = (own, over)
 
-        def finish(u):
-            own, over = state["pick", u]
-            res = ring.tile([P, NP], F32, name="res")
-            nc.vector.scalar_tensor_tensor(res[:], over[:], neg_std[:, u:u + 1], own[:], ALU.mult, ALU.add)
-            nc.sync.dma_start(out[P * u:P * u + P, :], res[:])
+        def finish(u, pieces):
+            n = NP // pieces
+            for k in range(pieces):
+                own, over = state["pick", u, k]
+                res = ring.tile([P, n], F32, name="res")
+                nc.vector.scalar_tensor_tensor(res[:], over[:], neg_std[:, u:u + 1], own[:, k * n:(k + 1) * n],
+                                               ALU.mult, ALU.add)
+                nc.sync.dma_start(out[P * u:P * u + P, k * n:(k + 1) * n], res[:])
 
+        scores(0, 1, N // 2, N // 2)
         for u in range(4):
-            pick(u)
+            if u < 3:
+                scores(u + 1, 0, 0, N)
+                scores(u + 1, 1, 0, N)
+            pick(u, 2 if u == 3 else 1)
             if u > 0:
-                finish(u - 1)
-        finish(3)
+                finish(u - 1, 1)
+        finish(3, 2)

@@ -18,8 +18,8 @@ ACT = mybir.ActivationFunctionType
 
 P = 128
 N = 512
-RELIEF = ()
-GWEAVE = ()
+RELIEF = (3, 5, 7, 9, 11)
+GWEAVE = (2, 3, 6, 7, 10, 11)
 
 
 def tile_list_breed_ring_scores_kernel(
@@ -30,8 +30,9 @@ def tile_list_breed_ring_scores_kernel(
     with ExitStack() as ctx:
         lists = ctx.enter_context(tc.tile_pool(name="lists", bufs=1))
         keep = ctx.enter_context(tc.tile_pool(name="keep", bufs=1))
-        ring = ctx.enter_context(tc.tile_pool(name="ring", bufs=4))
-        pair = ctx.enter_context(tc.tile_pool(name="pair", bufs=2))
+        ring = ctx.enter_context(tc.tile_pool(name="ring", bufs=6))
+        pair = ctx.enter_context(tc.tile_pool(name="pair", bufs=3))
+        tail = ctx.enter_context(tc.tile_pool(name="tail", bufs=3))
         psum = ctx.enter_context(tc.psum_pool(name="psum", bufs=2))
 
         offs_sb = lists.tile([P, S // 16], U16, name="offs_sb")
@@ -231,7 +232,9 @@ def tile_list_breed_ring_scores_kernel(
             if on_vector:
                 nc.vector.tensor_copy(dst, src)
             elif 4 * g + part in GWEAVE:
-                nc.gpsimd.tensor_scalar(dst, src, 1.0, 0.0, ALU.mult, ALU.add)
+                nc.gpsimd.tensor_scalar(state["h_wv", g][:, cols, :],
+                                        state["h_bf", g][:, :, cols].rearrange("p t n -> p n t"),
+                                        1.0, 0.0, ALU.mult, ALU.add)
             else:
                 nc.scalar.copy(dst, src)
 
@@ -256,23 +259,21 @@ def tile_list_breed_ring_scores_kernel(
         gather_v(0)
         gather_v(1)
         prepare_weights(0)
-        LEAD = 1
-        for i in range(LEAD + 1):
-            product_b(i)
-        for i in range(LEAD):
-            product_a(i)
-            first_sum(i)
-        product_c(0)
         last = len(steps) - 1
+        plan = {}
+        for i in range(last + 1):
+            lead_b, lead_a = (4, 4) if i in RELIEF else (2, 1)
+            plan.setdefault(max(i - lead_b, -1), []).append((product_b, i))
+            plan.setdefault(max(i - lead_a, -1), []).extend([(product_a, i), (first_sum, i)])
+        for stage, i in sorted(plan[-1], key=lambda item: item[1]):
+            stage(i)
+        product_c(0)
         for i in range(len(steps)):
             g, t, c0, n = steps[i]
-            if i == 4:
+            if i == 3:
                 prepare_weights(1)
-            if i + LEAD + 1 <= last:
-                product_b(i + LEAD + 1)
-            if i + LEAD <= last:
-                product_a(i + LEAD)
-                first_sum(i + LEAD)
+            for stage, j in sorted(plan.get(i, []), key=lambda item: item[1]):
+                stage(j)
             if i + 1 <= last:
                 product_c(i + 1)
             second_sum(i)
@@ -299,19 +300,19 @@ def tile_list_breed_ring_scores_kernel(
         nc.gpsimd.tensor_scalar(rest[:], std_sb[:], -1.0, 1.0, ALU.mult, ALU.add)
 
         def pick(u, pieces):
-            chal = ring.tile([P, NP], F32, name="chal")
+            chal = tail.tile([P, NP], F32, name="chal")
             nc.vector.tensor_copy(chal[:], e_sb[u][:].indirect(pos1_sb[:]))
-            own = ring.tile([P, NP], F32, name="own")
+            own = tail.tile([P, NP], F32, name="own")
             nc.scalar.activation(own[:], chal[:], ACT.Copy, scale=rest[:, u:u + 1])
             n = NP // pieces
             for k in range(pieces):
-                lead = ring.tile([P, n], F32, name="lead")
+                lead = tail.tile([P, n], F32, name="lead")
                 if pieces == 1:
                     places = pos2_sb[:]
                 else:
                     places = pos2_sb[:, k * n // 16:(k + 1) * n // 16]
                 nc.vector.tensor_tensor(lead[:], e_sb[u][:].indirect(places), chal[:, k * n:(k + 1) * n], ALU.subtract)
-                over = ring.tile([P, n], F32, name="over")
+                over = tail.tile([P, n], F32, name="over")
                 nc.scalar.activation(over[:], lead[:], ACT.Relu)
                 state["pick", u, k] = (own, over)
 
@@ -319,7 +320,7 @@ def tile_list_breed_ring_scores_kernel(
             n = NP // pieces
             for k in range(pieces):
                 own, over = state["pick", u, k]
-                res = ring.tile([P, n], F32, name="res")
+                res = tail.tile([P, n], F32, name="res")
                 nc.vector.scalar_tensor_tensor(res[:], over[:], neg_std[:, u:u + 1], own[:, k * n:(k + 1) * n],
                                                ALU.mult, ALU.add)
                 nc.sync.dma_start(out[P * u:P * u + P, k * n:(k + 1) * n], res[:])

from contextlib import ExitStack

import concourse.mybir as mybir

K, T, S, H, T3, S2, NP = 512, 4096, 1024, 1024, 2048, 512, 512
FLOPS = 2 * K * H * S * 3 + 2 * H * S2 * S

F32 = mybir.dt.float32
BF16 = mybir.dt.bfloat16
I32 = mybir.dt.int32
U32 = mybir.dt.uint32
U16 = mybir.dt.uint16
U8 = mybir.dt.uint8
FP8X4 = mybir.dt.float8_e4m3fn_x4
FP4X4 = mybir.dt.float4_e2m1fn_x4
ALU = mybir.AluOpType
ACT = mybir.ActivationFunctionType

P = 128
N = 512
RELIEF = (3, 5, 7, 9, 11)
GWEAVE = (2, 3, 6, 7, 10, 11)


def tile_list_breed_ring_scores_kernel(
    tc, tab_words, tab_scales, offs, w1, w4_words, w4_scales, w8_words, w8_scales,
    least, tab2_words, tab2_scales, offs2, pos1, pos2, std, out,
):
    nc = tc.nc
    with ExitStack() as ctx:
        lists = ctx.enter_context(tc.tile_pool(name="lists", bufs=1))
        keep = ctx.enter_context(tc.tile_pool(name="keep", bufs=1))
        ring = ctx.enter_context(tc.tile_pool(name="ring", bufs=6))
        pair = ctx.enter_context(tc.tile_pool(name="pair", bufs=3))
        tail = ctx.enter_context(tc.tile_pool(name="tail", bufs=3))
        psum = ctx.enter_context(tc.psum_pool(name="psum", bufs=2))

        offs_sb = lists.tile([P, S // 16], U16, name="offs_sb")
        offs2_sb = lists.tile([P, S2 // 16], U16, name="offs2_sb")
        pos1_sb = lists.tile([P, NP // 16], U16, name="pos1_sb")
        pos2_sb = lists.tile([P, NP // 16], U16, name="pos2_sb")

        def kept(shape, dtype, name):
            return keep.tile(shape, dtype, name=name, align_bytes=64)

        tab_w = kept([P, T], U32, "tab_w")
        tab_s = kept([P, T], U8, "tab_s")
        tab2_w = [kept([P, T3], U32, "tab2_w%d" % a) for a in range(2)]
        tab2_s = kept([P, T3], U8, "tab2_s")
        ws_raw = kept([P, H], U8, "ws_raw")
        w8_raw = [kept([P, N], I32, "w8_raw%d" % b) for b in range(2)]
        w4_raw = [kept([P, 2 * N], U8, "w4_raw%d" % b) for b in range(2)]
        w1_raw = [kept([P, 4, N // 2], F32, "w1_raw%d" % i) for i in range(4)]
        low = kept([P, 2, 4], F32, "low")
        neg_low = kept([P, 2, 4], F32, "neg_low")
        std_sb = kept([P, 4], F32, "std_sb")

        w8_hbm = w8_words[0].rearrange("p n t -> p (n t)").bitcast(I32)
        w4_hbm = w4_words[0].bitcast(I32)
        w1_hbm = w1.rearrange("(p j) c -> p j c", j=4)
        tab_s_hbm = tab_scales[0].bitcast(I32)
        tab2_s_hbm = tab2_scales.bitcast(I32)
        w4s_hbm = w4_scales[0].bitcast(I32)
        w8s_hbm = w8_scales[0].bitcast(I32)

        def load_weights(b):
            nc.sync.dma_start(w4_raw[b][:].bitcast(I32), w4_hbm[:, b * N // 2:(b + 1) * N // 2])
            nc.sync.dma_start(w8_raw[b][:], w8_hbm[:, b * N:(b + 1) * N])

        def load_w1(i):
            nc.sync.dma_start(w1_raw[i][:], w1_hbm[:, :, i * N // 2:(i + 1) * N // 2])

        def load_scale_rows(hbm, first, quads):
            for q in quads:
                nc.sync.dma_start(ws_raw[32 * q + first:32 * q + first + 4, :].bitcast(I32), hbm[4 * q:4 * q + 4, :])

        nc.vector.memset(ws_raw[:].bitcast(I32), 0)
        nc.gpsimd.memset(tab2_s[:].bitcast(I32), 0)
        nc.sync.dma_start(offs_sb[:], offs)
        for q in range(4):
            nc.sync.dma_start(tab_s[32 * q:32 * q + 32, :].bitcast(I32),
                              tab_s_hbm[4 * q:4 * q + 4, :].partition_broadcast(8))
        load_scale_rows(w4s_hbm, 0, (0, 1))
        nc.sync.dma_start(tab_w[:].bitcast(I32), tab_words[0].rearrange("p n t -> p (n t)").bitcast(I32))
        load_scale_rows(w4s_hbm, 0, (2, 3))
        load_scale_rows(w8s_hbm, 4, (0, 1, 2, 3))
        load_w1(0)
        load_w1(1)
        load_weights(0)
        nc.sync.dma_start(low[:], least.rearrange("(b p t) -> p b t", b=2, t=4))
        load_w1(2)
        load_w1(3)
        load_weights(1)
        nc.sync.dma_start(offs2_sb[:], offs2)
        for q in range(4):
            nc.sync.dma_start(tab2_s[32 * q:32 * q + 8, :].bitcast(I32), tab2_s_hbm[:, 4 * q:4 * q + 4, :])
        for a in range(2):
            nc.sync.dma_start(tab2_w[a][:].bitcast(I32), tab2_words[a].rearrange("p n t -> p (n t)").bitcast(I32))
        nc.sync.dma_start(pos1_sb[:], pos1)
        nc.sync.dma_start(pos2_sb[:], pos2)
        with nc.allow_non_contiguous_dma(reason="one value of std for each partition"):
            nc.sync.dma_start(std_sb[:], std.rearrange("(u p) -> p u", p=P))

        v_s = kept([P, S], U8, "v_s")
        nc.vector.tensor_copy(v_s[:], tab_s[:].indirect(offs_sb[:]))
        v_w = [kept([P, N], U32, "v_w%d" % jc) for jc in range(2)]

        def gather_v(jc):
            nc.vector.tensor_copy(v_w[jc][:], tab_w[:].indirect(offs_sb[:, 32 * jc:32 * jc + 32]))

        w1_bf = [kept([P, 4, P, 4], BF16, "w1_bf%d" % b) for b in range(2)]
        w1_c = [kept([P, N], U32, "w1_c%d" % b) for b in range(2)]
        w1_s = [kept([P, N], U8, "w1_s%d" % b) for b in range(2)]
        w8_p = [kept([P, 4, P], I32, "w8_p%d" % b) for b in range(2)]
        w4_p = [kept([P, 4, P], U16, "w4_p%d" % b) for b in range(2)]
        ws_p = [kept([P, 4, P], U8, "ws_p%d" % b) for b in range(2)]

        def prepare_weights(b):
            for part in range(4):
                dst = w1_bf[b][:, :, 32 * part:32 * part + 32, :].rearrange("p t m j -> p m j t")
                src = w1_raw[2 * b + part // 2][:, :, 128 * (part % 2):128 * (part % 2) + 128]
                src = src.rearrange("p j (m t) -> p m j t", t=4)
                if b == 0 and part == 3:
                    nc.vector.tensor_copy(dst, src)
                elif b == 1 and False:
                    nc.gpsimd.tensor_scalar(dst, src, 1.0, 0.0, ALU.mult, ALU.add)
                else:
                    nc.scalar.copy(dst, src)
            nc.vector.tensor_copy(ws_p[b][:].rearrange("p t q -> p q t"),
                                  ws_raw[:, b * N:(b + 1) * N].rearrange("p (q t) -> p q t", t=4))
            nc.vector.tensor_copy(w4_p[b][:].rearrange("p t q -> p q t"),
                                  w4_raw[b][:].bitcast(U16).rearrange("p (q t) -> p q t", t=4))
            calls = 2 - b
            wide = N // calls
            for k in range(calls):
                nc.vector.quantize_mx(out=w1_c[b][:, k * wide:(k + 1) * wide].bitcast(FP8X4),
                                      scales=w1_s[b][:, k * wide:(k + 1) * wide],
                                      in_=w1_bf[b][:].rearrange("p t m j -> p (t m j)")[:, 4 * k * wide:4 * (k + 1) * wide])
                if k == 0:
                    nc.vector.tensor_copy(w8_p[b][:].rearrange("p t q -> p q t"),
                                          w8_raw[b][:].rearrange("p (q t) -> p q t", t=4))

        v2_w = {(a, 0): kept([P, S2 // 2], U32, "v2_w%d" % a) for a in range(2)}
        v2_s = kept([P, S2], U8, "v2_s")

        def gather_v2():
            nc.vector.tensor_copy(v2_s[:], tab2_s[:].indirect(offs2_sb[:]))
            for a in range(2):
                nc.vector.tensor_copy(v2_w[a, 0][:], tab2_w[a][:].indirect(offs2_sb[:, 0:16]))

        def gather_v2_late():
            late = keep.tile([P, 2, S2 // 2], U32, name="v2_late", tag="last_woven", align_bytes=64)
            for a in range(2):
                v2_w[a, 1] = late[:, a, :]
                nc.vector.tensor_copy(late[:, a, :], tab2_w[a][:].indirect(offs2_sb[:, 16:32]))

        h_c = [kept([P, N], U32, "h_c%d" % g) for g in range(4)]
        h_s = [kept([P, N], U8, "h_s%d" % g) for g in range(4)]
        e_sb = [kept([P, S], F32, "e_sb%d" % u) for u in range(4)]

        steps = [(g, t, 0, N) for g in range(3) for t in range(4)]
        steps = steps + [(3, t, c0, N // 2) for c0 in (0, N // 2) for t in range(4)]
        state = {}

        def moving(i):
            g, t, c0, n = steps[i]
            jc = g % 2
            return v_w[jc][:, c0:c0 + n].bitcast(FP8X4), v_s[:, jc * N + c0:jc * N + c0 + n]

        def product_b(i):
            g, t, c0, n = steps[i]
            b = g // 2
            rhs, rhs_s = moving(i)
            bank_b = psum.tile([P, n], F32, name="bank_b")
            nc.tensor.matmul_mx(out=bank_b[:], lhsT=w4_p[b][:, t, :].bitcast(FP4X4), lhsT_scale=ws_p[b][:, t, :],
                                rhs=rhs, rhs_scale=rhs_s, start=True, stop=True)
            b_sb = ring.tile([P, n], F32, name="b_sb")
            if i in RELIEF:
                nc.scalar.activation(b_sb[:], bank_b[:], ACT.Identity, bias=low[:, b, t:t + 1])
            else:
                nc.scalar.copy(b_sb[:], bank_b[:])
            state["b", i] = b_sb

        def product_a(i):
            g, t, c0, n = steps[i]
            b = g // 2
            cols = slice(P * t, P * t + P)
            rhs, rhs_s = moving(i)
            bank_a = psum.tile([P, n], F32, name="bank_a")
            nc.tensor.matmul_mx(out=bank_a[:], lhsT=w1_c[b][:, cols].bitcast(FP8X4), lhsT_scale=w1_s[b][:, cols],
                                rhs=rhs, rhs_scale=rhs_s, start=True, stop=True)
            state["a", i] = bank_a

        def product_c(i):
            g, t, c0, n = steps[i]
            b = g // 2
            rhs, rhs_s = moving(i)
            bank_c = psum.tile([P, n], F32, name="bank_c")
            nc.tensor.matmul_mx(out=bank_c[:], lhsT=w8_p[b][:, t, :].bitcast(FP8X4), lhsT_scale=ws_p[b][4:P, t, :],
                                rhs=rhs, rhs_scale=rhs_s, start=True, stop=True)
            state["c", i] = bank_c

        def first_sum(i):
            g, t, c0, n = steps[i]
            b = g // 2
            run = ring.tile([P, n], F32, name="run")
            if i in RELIEF:
                above = ring.tile([P, n], F32, name="above")
                nc.scalar.activation(above[:], state["a", i][:], ACT.Relu, bias=neg_low[:, b, t:t + 1])
                nc.gpsimd.tensor_tensor(run[:], above[:], state["b", i][:], ALU.add)
            else:
                nc.vector.scalar_tensor_tensor(run[:], state["a", i][:], low[:, b, t:t + 1], state["b", i][:],
                                               ALU.max, ALU.add)
            state["run", i] = run

        def second_sum(i):
            g, t, c0, n = steps[i]
            b = g // 2
            if t == 0 and c0 == 0:
                state["h_bf", g] = pair.tile([P, 4, N], BF16, name="h_bf")
            nc.vector.scalar_tensor_tensor(state["h_bf", g][:, t, c0:c0 + n], state["run", i][:], low[:, b, t:t + 1],
                                           state["c", i][:], ALU.max, ALU.add)

        def weave(g, part, on_vector):
            if part == 0 and g == 3:
                state["h_wv", g] = keep.tile([P, N, 4], BF16, name="h_wv_last", tag="last_woven", align_bytes=64)
            elif part == 0:
                state["h_wv", g] = pair.tile([P, N, 4], BF16, name="h_wv", align_bytes=64)
            cols = slice(P * part, P * part + P)
            dst = state["h_wv", g][:, cols, :].rearrange("p (c i) t -> p c t i", i=4)
            src = state["h_bf", g][:, :, cols].rearrange("p t (c i) -> p c t i", i=4)
            if on_vector:
                nc.vector.tensor_copy(dst, src)
            elif 4 * g + part in GWEAVE:
                nc.gpsimd.tensor_scalar(state["h_wv", g][:, cols, :],
                                        state["h_bf", g][:, :, cols].rearrange("p t n -> p n t"),
                                        1.0, 0.0, ALU.mult, ALU.add)
            else:
                nc.scalar.copy(dst, src)

        def quantize_h(g, c0, n):
            nc.vector.quantize_mx(out=h_c[g][:, c0:c0 + n].bitcast(FP8X4), scales=h_s[g][:, c0:c0 + n],
                                  in_=state["h_wv", g][:, c0:c0 + n, :].rearrange("p n t -> p (n t)"))

        def score_pass(bank, u, jc, c0, n, a):
            cols = slice(P * u, P * u + P)
            g = 2 * a + jc
            nc.tensor.matmul_mx(out=bank[:], lhsT=v2_w[a, u // 2][:, P * (u % 2):P * (u % 2) + P].bitcast(FP8X4),
                                lhsT_scale=v2_s[4 * a:P, cols], rhs=h_c[g][:, c0:c0 + n].bitcast(FP8X4),
                                rhs_scale=h_s[g][:, c0:c0 + n], start=(a == 0), stop=(a == 1))

        def scores(u, jc, c0, n):
            bank_e = psum.tile([P, n], F32, name="bank_e")
            score_pass(bank_e, u, jc, c0, n, 0)
            score_pass(bank_e, u, jc, c0, n, 1)
            nc.scalar.copy(e_sb[u][:, jc * N + c0:jc * N + c0 + n], bank_e[:])

        nc.gpsimd.tensor_scalar(neg_low[:], low[:], -1.0, 0.0, ALU.mult, ALU.add)
        gather_v(0)
        gather_v(1)
        prepare_weights(0)
        last = len(steps) - 1
        plan = {}
        for i in range(last + 1):
            lead_b, lead_a = (4, 4) if i in RELIEF else (2, 1)
            plan.setdefault(max(i - lead_b, -1), []).append((product_b, i))
            plan.setdefault(max(i - lead_a, -1), []).extend([(product_a, i), (first_sum, i)])
        for stage, i in sorted(plan[-1], key=lambda item: item[1]):
            stage(i)
        product_c(0)
        for i in range(len(steps)):
            g, t, c0, n = steps[i]
            if i == 3:
                prepare_weights(1)
            for stage, j in sorted(plan.get(i, []), key=lambda item: item[1]):
                stage(j)
            if i + 1 <= last:
                product_c(i + 1)
            second_sum(i)
            if g > 0 and c0 == 0:
                weave(g - 1, t, False)
                if t == 3:
                    quantize_h(g - 1, 0, N)
            if c0 > 0 and t < 2:
                weave(3, t, False)
            if c0 > 0 and t == 2:
                quantize_h(3, 0, N // 2)
                scores(0, 0, 0, N)
                scores(0, 1, 0, N // 2)
            if i == 9:
                gather_v2()
        weave(3, 2, True)
        weave(3, 3, False)
        quantize_h(3, N // 2, N // 2)
        gather_v2_late()

        neg_std = kept([P, 4], F32, "neg_std")
        rest = kept([P, 4], F32, "rest")
        nc.gpsimd.tensor_scalar(neg_std[:], std_sb[:], -1.0, 0.0, ALU.mult, ALU.add)
        nc.gpsimd.tensor_scalar(rest[:], std_sb[:], -1.0, 1.0, ALU.mult, ALU.add)

        def pick(u, pieces):
            chal = tail.tile([P, NP], F32, name="chal")
            nc.vector.tensor_copy(chal[:], e_sb[u][:].indirect(pos1_sb[:]))
            own = tail.tile([P, NP], F32, name="own")
            nc.scalar.activation(own[:], chal[:], ACT.Copy, scale=rest[:, u:u + 1])
            n = NP // pieces
            for k in range(pieces):
                lead = tail.tile([P, n], F32, name="lead")
                if pieces == 1:
                    places = pos2_sb[:]
                else:
                    places = pos2_sb[:, k * n // 16:(k + 1) * n // 16]
                nc.vector.tensor_tensor(lead[:], e_sb[u][:].indirect(places), chal[:, k * n:(k + 1) * n], ALU.subtract)
                over = tail.tile([P, n], F32, name="over")
                nc.scalar.activation(over[:], lead[:], ACT.Relu)
                state["pick", u, k] = (own, over)

        def finish(u, pieces):
            n = NP // pieces
            for k in range(pieces):
                own, over = state["pick", u, k]
                res = tail.tile([P, n], F32, name="res")
                nc.vector.scalar_tensor_tensor(res[:], over[:], neg_std[:, u:u + 1], own[:, k * n:(k + 1) * n],
                                               ALU.mult, ALU.add)
                nc.sync.dma_start(out[P * u:P * u + P, k * n:(k + 1) * n], res[:])

        scores(0, 1, N // 2, N // 2)
        for u in range(4):
            if u < 3:
                scores(u + 1, 0, 0, N)
                scores(u + 1, 1, 0, N)
            pick(u, 2 if u == 3 else 1)
            if u > 0:
                finish(u - 1, 1)
        finish(3, 2)
